import numpy as np
import ml_dtypes


def mxq(x, axis, fmt="e4m3"):
    dtype, down = {"e4m3": (ml_dtypes.float8_e4m3fn, 7), "e5m2": (ml_dtypes.float8_e5m2, 14)}[fmt]
    v = np.moveaxis(np.asarray(x, np.float32).astype(ml_dtypes.bfloat16).astype(np.float64), axis, -1)
    blocks = v.reshape(v.shape[:-1] + (-1, 32))
    amax = np.abs(blocks).max(-1, keepdims=True)
    byte = np.maximum(np.where(amax > 0, np.frexp(amax)[1] - 1 + 127, 0) - down, 1)
    scale = np.exp2(byte - 127.0)
    codes = (blocks / scale).astype(np.float32).astype(dtype).astype(np.float64)
    return np.moveaxis((codes * scale).reshape(v.shape), -1, axis)


WIDE = False


def mx_kscale(k):
    if not WIDE:
        return np.ones(k)
    levels = np.array([10, -10, 5, -5, 0])
    if k % 512:
        return np.exp2(np.random.permutation(np.resize(levels, k // 32))).repeat(32)
    a = np.empty((k // 512, 16))
    for p in range(k // 512):
        a[p, :8] = np.random.permutation(np.resize(levels, 8))
        for g in range(8):
            far = levels[np.abs(levels - a[p, g]) >= 10]
            a[p, g + 8] = far[np.random.randint(len(far))]
    return np.exp2(a.ravel()).repeat(32)


def f64(x):
    return np.asarray(x).astype(np.float64)


def striped(idx):
    return np.tile(idx.reshape(-1, 16).T, (8, 1)).astype(np.uint16)


def unstriped(offs):
    return offs[:16].T.reshape(-1).astype(np.int64)


def striped8(idx):
    return np.concatenate([x.reshape(-1, 16).T for x in idx]).astype(np.uint16)


def runs(offs, k):
    lists = np.stack([offs[16 * r : 16 * r + 16].T.reshape(-1) for r in range(8)]).astype(np.int64)
    return lists[np.arange(k) % 512 // 64]


def pack_weight(w):
    k, n = w.shape
    w = f64(np.asarray(w, np.float32).astype(ml_dtypes.bfloat16)).reshape(k // 32, 32, n)
    amax = np.abs(w).max(1)
    byte = np.clip(np.where(amax > 0, np.frexp(amax)[1] - 1 + 127 - 7, 1), 1, 254)
    scaled = (w * np.exp2(127.0 - byte)[:, None, :]).reshape(k, n).astype(np.float32)
    words = np.ascontiguousarray(scaled.reshape(k // 512, 128, 4, n).transpose(0, 1, 3, 2)).astype(ml_dtypes.float8_e4m3fn).view(np.uint8)
    return words, np.ascontiguousarray(byte.astype(np.uint8).reshape(k // 512, 16, n))


def unpack_weight(words, scales):
    g, p, n, _ = words.shape
    vals = np.ascontiguousarray(words).view(ml_dtypes.float8_e4m3fn).astype(np.float64) * np.repeat(np.exp2(scales.astype(np.float64) - 127.0), 8, axis=1)[..., None]
    return vals.transpose(0, 1, 3, 2).reshape(g * 512, n)


K, T, S, H, W, C = 512, 2048, 512, 512, 256, 512


def setup_inputs():
    n = np.random.standard_normal
    s = mx_kscale(K)[:, None]
    packed_xT = pack_weight(n((K, T)) * s)
    perm = np.stack([np.random.permutation(S) for _ in range(8)])
    return {
        "x_words": packed_xT[0],
        "x_scales": packed_xT[1],
        "w1": (n((K, H)) / np.sqrt(K) / s).astype(np.float32),
        "gs": (np.random.uniform(0.5, 1.5, (K, 1)) / s).astype(np.float32),
        "offs": striped(np.random.permutation(T)[:S]),
        "n1": striped8(perm[:, :W]),
        "n2": striped8(perm[:, W:]),
        "ca": striped(np.random.permutation(T)[:C]),
        "hc": striped8(np.random.randint(0, T, (8, C))),
        "n3": striped(np.random.permutation(S)[:W]),
        "n4": striped(np.random.permutation(S)[:W]),
    }


def reference(x_words, x_scales, w1, gs, offs, n1, n2, ca, hc, n3, n4):
    x_hc = unpack_weight(x_words, x_scales)[np.arange(K)[:, None], runs(hc, K)]
    xq = unpack_weight(x_words, x_scales)[:, unstriped(offs)]
    y = mxq(f64(w1), 0, "e4m3").T @ xq
    pa = y[np.arange(H)[:, None], runs(n1, H)]
    pb = y[np.arange(H)[:, None], runs(n2, H)]
    rb = pa - pb
    ra = 0.75 * (pa + pb)
    ds = np.zeros((H, S))
    ds[np.arange(H)[:, None], runs(n1, H)] = ra
    dt = ds.copy()
    dt[np.arange(H)[:, None], runs(n2, H)] = rb
    z = f64(gs) * dt
    zq = mxq(z, 0, "e4m3")
    b = 0.0625 * (x_hc.T @ zq)
    x_ca = unpack_weight(x_words, x_scales)[:, unstriped(ca)]
    a = 0.0625 * (x_ca.T @ zq)
    ra2 = b[:, unstriped(n4)] - (0.5 * a[:, unstriped(n3)])
    out = a.copy()
    out[:, unstriped(n3)] = ra2
    return out

@@ -1,0 +1,248 @@
+from contextlib import ExitStack
+
+import concourse.mybir as mybir
+
+K, T, S, H, W, C = 512, 2048, 512, 512, 256, 512
+FLOPS = 3 * 2 * 512 * 512 * 512
+
+F32 = mybir.dt.float32
+BF16 = mybir.dt.bfloat16
+I32 = mybir.dt.int32
+U32 = mybir.dt.uint32
+U16 = mybir.dt.uint16
+U8 = mybir.dt.uint8
+FP8X4 = mybir.dt.float8_e4m3fn_x4
+COPY = mybir.ActivationFunctionType.Copy
+ADD = mybir.AluOpType.add
+MULT = mybir.AluOpType.mult
+
+P = 128
+PACK = 4
+ROW_ORDER = (0, 2, 3, 1)
+V_COLS = 344
+
+
+def tile_picked_cdhputbhaar_none_p_kernel(
+    tc, x_words, x_scales, w1, gs, offs, n1, n2, ca, hc, n3, n4, out
+):
+    nc = tc.nc
+    with ExitStack() as ctx:
+        keep = ctx.enter_context(tc.tile_pool(name="keep", bufs=1))
+        ring = ctx.enter_context(tc.tile_pool(name="ring", bufs=4))
+        psum = ctx.enter_context(tc.psum_pool(name="psum", bufs=1))
+
+        def load_list(src, name):
+            lst = keep.tile(list(src.shape), U16, name=name)
+            nc.sync.dma_start(lst[:], src)
+            return lst
+
+        offs_l = load_list(offs, "offs_l")
+        hc_l = load_list(hc, "hc_l")
+        scale_table = keep.tile([P, T], U8, name="scale_table", align_bytes=64)
+        table = scale_table[:].bitcast(I32)
+        nc.vector.memset(table[:, :320], 0)
+        nc.gpsimd.memset(table[:, 320:], 0)
+        rows = x_scales[0].bitcast(I32)
+        for s in range(2):
+            nc.scalar.dma_start(table[s:P:16, :], rows[s:16:2, :])
+        for s in range(2, 4):
+            nc.sync.dma_start(table[s:P:32, :], rows[s:16:4, :])
+        w_raw = keep.tile([P, PACK, H], F32, name="w_raw")
+        nc.sync.dma_start(w_raw[:], w1.rearrange("(p j) c -> p j c", j=PACK))
+        ca_l = load_list(ca, "ca_l")
+        word_table = keep.tile([P, T], U32, name="word_table", align_bytes=64)
+        nc.sync.dma_start(
+            word_table[:].bitcast(I32), x_words[0].rearrange("p n t -> p (n t)").bitcast(I32)
+        )
+        gain = keep.tile([P, PACK], F32, name="gain")
+        nc.sync.dma_start(gain[:], gs.rearrange("(p t) o -> p (t o)", t=PACK))
+        n1_l = load_list(n1, "n1_l")
+        n2_l = load_list(n2, "n2_l")
+        n3_l = load_list(n3, "n3_l")
+        n4_l = load_list(n4, "n4_l")
+
+        def pick(source, lst, dtype, name, pieces=1):
+            got = keep.tile([P, S], dtype, name=name, align_bytes=64)
+            return gather(got, source, lst, pieces)
+
+        def gather(got, source, lst, pieces=1):
+            n = S // pieces
+            for i in range(pieces):
+                nc.vector.tensor_copy(
+                    got[:, i * n : (i + 1) * n],
+                    source[:].indirect(lst[:, i * n // 16 : (i + 1) * n // 16]),
+                )
+            return got
+
+        xq_scales = pick(scale_table, offs_l, U8, "xq_scales")
+        hc_picked = pick(scale_table, hc_l, U8, "hc_picked")
+        ca_scales = pick(scale_table, ca_l, U8, "ca_scales")
+
+        hc_scales = keep.tile([P, C], U8, name="hc_scales", align_bytes=64)
+        nc.vector.memset(hc_scales[:].bitcast(I32), 0)
+        for r in range(4):
+            first = r + 14 * (r // 2)
+            nc.sync.dma_start(
+                hc_scales[r:P:32, :].bitcast(I32), hc_picked[first:P:32, :].bitcast(I32)
+            )
+
+        w_bf = keep.tile([P, PACK, P, PACK], BF16, name="w_bf", tag="w_then_words", align_bytes=64)
+        nc.scalar.copy(
+            w_bf[:].rearrange("p t m j -> p m j t"),
+            w_raw[:].rearrange("p j (m t) -> p m j t", t=PACK),
+        )
+        w_words = keep.tile([P, H], U32, name="w_words", align_bytes=64)
+        w_scales = keep.tile([P, H], U8, name="w_scales", align_bytes=64)
+        w_flat = w_bf[:].rearrange("p t m j -> p (t m j)")
+        for lo, hi in ((0, P), (P, H)):
+            nc.vector.quantize_mx(
+                out=w_words[:, lo:hi].bitcast(FP8X4),
+                scales=w_scales[:, lo:hi],
+                in_=w_flat[:, PACK * lo : PACK * hi],
+            )
+        xq_words = pick(word_table, offs_l, U32, "xq_words", pieces=2)
+        cand_words = keep.tile([P, 2 * C], U32, name="cand_words", tag="w_then_words", align_bytes=64)
+        ca_words = gather(cand_words[:, :C], word_table, ca_l)
+        hc_words = gather(cand_words[:, C:], word_table, hc_l)
+
+        halves = (slice(0, S // 2), slice(S // 2, S))
+        whole = (slice(0, S),)
+
+        def product(acc, words, scales, cols, mov_words, mov_scales, part):
+            nc.tensor.matmul_mx(
+                out=acc[:, part],
+                lhsT=words[:, cols].bitcast(FP8X4),
+                lhsT_scale=scales[:, cols],
+                rhs=mov_words[:, part].bitcast(FP8X4),
+                rhs_scale=mov_scales[:, part],
+                start=True,
+                stop=True,
+            )
+
+        def project(step):
+            t = ROW_ORDER[step]
+            cols = slice(t * P, (t + 1) * P)
+            y = keep.tile([P, S], F32, name="y", tag=f"y{step}", align_bytes=64)
+            for k, part in enumerate(halves if step == 0 else whole):
+                y_ps = psum.tile([P, S], F32, name="y_ps", tag=f"y_ps{k}", bufs=1)
+                product(y_ps, w_words, w_scales, cols, xq_words, xq_scales, part)
+                nc.scalar.activation(y[:, part], y_ps[:, part], COPY, scale=gain[:, t : t + 1])
+            pa = ring.tile([P, W], F32, name="pa")
+            nc.scalar.activation(pa[:], y[:].indirect(n1_l[:]), COPY)
+            neg_pb = ring.tile([P, W], F32, name="neg_pb")
+            nc.scalar.activation(neg_pb[:], y[:].indirect(n2_l[:]), COPY, scale=-1.0)
+            return pa, neg_pb
+
+        def three_quarters(pair, tag):
+            q = keep.tile([P, 2, W], F32, name="q", tag=tag, align_bytes=64)
+            nc.scalar.activation(q[:, 0, :], pair[0][:], COPY, scale=0.75)
+            nc.scalar.activation(q[:, 1, :], pair[1][:], COPY, scale=-0.75)
+            return q
+
+        pairs = [project(0)]
+        sums = [three_quarters(pairs[0], "q0")]
+        pairs.append(project(1))
+        pairs.append(project(2))
+        sums.append(three_quarters(pairs[1], "y2"))
+        sums.append(three_quarters(pairs[2], "q2"))
+        pairs.append(project(3))
+        sums.append(three_quarters(pairs[3], "q3"))
+
+        z_bf = keep.tile([P, S, PACK], BF16, name="z_bf", tag="y3", align_bytes=64)
+        z_tiles = {}
+
+        def put_differences(step):
+            z = ring.tile([P, S], F32, name="z", bufs=3)
+            nc.vector.tensor_tensor(z[:].indirect(n2_l[:]), pairs[step][0][:], pairs[step][1][:], ADD)
+            z_tiles[step] = z
+
+        def put_sums(step):
+            z, t = z_tiles[step], ROW_ORDER[step]
+            nc.vector.tensor_tensor(z[:].indirect(n1_l[:]), sums[step][:, 0, :], sums[step][:, 1, :], ADD)
+            if step < 3:
+                nc.scalar.copy(z_bf[:, :, t], z[:])
+            else:
+                nc.vector.tensor_copy(z_bf[:, : S // 2, t], z[:, : S // 2])
+                nc.vector.tensor_copy(z_bf[:, S // 2 : V_COLS, t], z[:, S // 2 : V_COLS])
+                nc.scalar.copy(z_bf[:, V_COLS:, t], z[:, V_COLS:])
+
+        put_differences(0)
+        put_sums(0)
+        put_differences(1)
+        put_differences(2)
+        put_sums(1)
+        put_sums(2)
+        put_differences(3)
+        put_sums(3)
+
+        z_words = keep.tile([P, S], U32, name="z_words", align_bytes=64)
+        z_scales = keep.tile([P, S], U8, name="z_scales", align_bytes=64)
+        for part in halves:
+            nc.vector.quantize_mx(
+                out=z_words[:, part].bitcast(FP8X4),
+                scales=z_scales[:, part],
+                in_=z_bf[:, part, :].rearrange("p s t -> p (s t)"),
+            )
+
+        blocks = [slice(i * P, (i + 1) * P) for i in range(C // P)]
+        sides = {"a": (ca_words, ca_scales), "b": (hc_words, hc_scales)}
+        acc = {}
+
+        def bank(side, i, tag):
+            acc[side, i] = psum.tile([P, S], F32, name="acc", tag=tag, bufs=1)
+
+        def score(side, i, part):
+            product(acc[side, i], sides[side][0], sides[side][1], blocks[i], z_words, z_scales, part)
+
+        order = [("a", 0), ("b", 0), ("a", 1), ("b", 1), ("a", 2), ("a", 3), ("b", 2), ("b", 3)]
+        for k, (side, i) in enumerate(order):
+            bank(side, i, f"y_ps{k}")
+        for part in halves:
+            score("a", 0, part)
+            score("b", 0, part)
+        for side, i in order[2:]:
+            score(side, i, whole[0])
+
+        a_sb, b_sb, half_a = {}, {}, {}
+
+        def copy_a(i):
+            a_sb[i] = ring.tile([P, S], F32, name="a")
+            nc.scalar.activation(a_sb[i][:], acc["a", i][:], COPY, scale=0.0625)
+
+        def fetch_a(i):
+            half_a[i] = ring.tile([P, W], F32, name="half")
+            nc.scalar.activation(half_a[i][:], a_sb[i][:].indirect(n3_l[:]), COPY, scale=-0.5)
+
+        def copy_b(i):
+            b_sb[i] = ring.tile([P, S], F32, name="b")
+            if i == 1:
+                nc.scalar.activation(b_sb[i][:], acc["b", i][:], COPY, scale=0.0625)
+            else:
+                nc.vector.tensor_scalar(b_sb[i][:], acc["b", i][:], 0.0625, None, MULT)
+
+        def finish(i):
+            got_b = ring.tile([P, W], F32, name="got_b")
+            if i in (0, C // P - 1):
+                nc.vector.tensor_copy(got_b[:], b_sb[i][:].indirect(n4_l[:]))
+                nc.vector.tensor_tensor(a_sb[i][:].indirect(n3_l[:]), got_b[:], half_a[i][:], ADD)
+            else:
+                nc.vector.tensor_tensor(got_b[:], b_sb[i][:].indirect(n4_l[:]), half_a[i][:], ADD)
+                nc.scalar.activation(a_sb[i][:].indirect(n3_l[:]), got_b[:], COPY)
+            nc.sync.dma_start(out[blocks[i], :], a_sb[i][:])
+
+        copy_a(0)
+        fetch_a(0)
+        copy_b(0)
+        finish(0)
+        copy_a(1)
+        copy_b(1)
+        fetch_a(1)
+        for i in (2, 3):
+            copy_a(i)
+        for i in (2, 3):
+            fetch_a(i)
+        finish(1)
+        for i in (2, 3):
+            copy_b(i)
+        for i in (2, 3):
+            finish(i)

@@ -40,15 +40,18 @@ def tile_picked_cdhputbhaar_none_p_kernel(
         hc_l = load_list(hc, "hc_l")
         scale_table = keep.tile([P, T], U8, name="scale_table", align_bytes=64)
         table = scale_table[:].bitcast(I32)
-        nc.vector.memset(table[:, :320], 0)
-        nc.gpsimd.memset(table[:, 320:], 0)
+        nc.vector.memset(table, 0)
         rows = x_scales[0].bitcast(I32)
         for s in range(2):
             nc.scalar.dma_start(table[s:P:16, :], rows[s:16:2, :])
         for s in range(2, 4):
             nc.sync.dma_start(table[s:P:32, :], rows[s:16:4, :])
-        w_raw = keep.tile([P, PACK, H], F32, name="w_raw")
-        nc.sync.dma_start(w_raw[:], w1.rearrange("(p j) c -> p j c", j=PACK))
+        w_rows = w1.rearrange("(p j) c -> p j c", j=PACK)
+        w_raw = []
+        for h in range(2):
+            part = keep.tile([P, PACK, H // 2], F32, name=f"w_raw{h}")
+            nc.sync.dma_start(part[:], w_rows[:, :, h * (H // 2) : (h + 1) * (H // 2)])
+            w_raw.append(part)
         ca_l = load_list(ca, "ca_l")
         word_table = keep.tile([P, T], U32, name="word_table", align_bytes=64)
         nc.sync.dma_start(
@@ -87,10 +90,11 @@ def tile_picked_cdhputbhaar_none_p_kernel(
             )
 
         w_bf = keep.tile([P, PACK, P, PACK], BF16, name="w_bf", tag="w_then_words", align_bytes=64)
-        nc.scalar.copy(
-            w_bf[:].rearrange("p t m j -> p m j t"),
-            w_raw[:].rearrange("p j (m t) -> p m j t", t=PACK),
-        )
+        for h in range(2):
+            nc.scalar.copy(
+                w_bf[:, :, h * (P // 2) : (h + 1) * (P // 2), :].rearrange("p t m j -> p m j t"),
+                w_raw[h][:].rearrange("p j (m t) -> p m j t", t=PACK),
+            )
         w_words = keep.tile([P, H], U32, name="w_words", align_bytes=64)
         w_scales = keep.tile([P, H], U8, name="w_scales", align_bytes=64)
         w_flat = w_bf[:].rearrange("p t m j -> p (t m j)")
@@ -187,62 +191,67 @@ def tile_picked_cdhputbhaar_none_p_kernel(
         blocks = [slice(i * P, (i + 1) * P) for i in range(C // P)]
         sides = {"a": (ca_words, ca_scales), "b": (hc_words, hc_scales)}
         acc = {}
-
-        def bank(side, i, tag):
-            acc[side, i] = psum.tile([P, S], F32, name="acc", tag=tag, bufs=1)
-
-        def score(side, i, part):
-            product(acc[side, i], sides[side][0], sides[side][1], blocks[i], z_words, z_scales, part)
-
-        order = [("a", 0), ("b", 0), ("a", 1), ("b", 1), ("a", 2), ("a", 3), ("b", 2), ("b", 3)]
-        for k, (side, i) in enumerate(order):
-            bank(side, i, f"y_ps{k}")
-        for part in halves:
-            score("a", 0, part)
-            score("b", 0, part)
-        for side, i in order[2:]:
-            score(side, i, whole[0])
+        jobs = [("a", 0, part) for part in halves] + [("b", 0, part) for part in halves]
+        jobs.extend((side, i, whole[0]) for side, i in (("a", 1), ("b", 2), ("b", 1), ("a", 2), ("a", 3), ("b", 3)))
+        for k, (side, i, part) in enumerate(jobs):
+            bank = psum.tile([P, S], F32, name="acc", tag=f"y_ps{k % 8}", bufs=1)
+            product(bank, sides[side][0], sides[side][1], blocks[i], z_words, z_scales, part)
+            acc.setdefault((side, i), []).append((bank, part))
 
         a_sb, b_sb, half_a = {}, {}, {}
 
         def copy_a(i):
             a_sb[i] = ring.tile([P, S], F32, name="a")
-            nc.scalar.activation(a_sb[i][:], acc["a", i][:], COPY, scale=0.0625)
+            for bank, part in acc["a", i]:
+                nc.scalar.activation(a_sb[i][:, part], bank[:, part], COPY, scale=0.0625)
 
         def fetch_a(i):
             half_a[i] = ring.tile([P, W], F32, name="half")
             nc.scalar.activation(half_a[i][:], a_sb[i][:].indirect(n3_l[:]), COPY, scale=-0.5)
 
         def copy_b(i):
-            b_sb[i] = ring.tile([P, S], F32, name="b")
-            if i == 1:
-                nc.scalar.activation(b_sb[i][:], acc["b", i][:], COPY, scale=0.0625)
+            b_sb[i] = ring.tile([P, S], F32, name="b", tag=f"b{i % 2}", bufs=1)
+            for bank, part in acc["b", i]:
+                if i == 1:
+                    nc.scalar.activation(b_sb[i][:, part], bank[:, part], COPY, scale=0.0625)
+                else:
+                    nc.vector.tensor_scalar(b_sb[i][:, part], bank[:, part], 0.0625, None, MULT)
+
+        got_b = {}
+        on_vector = (0, C // P - 1)
+
+        def fetch_b(i):
+            got_b[i] = ring.tile([P, W], F32, name="got_b")
+            if i in on_vector:
+                nc.vector.tensor_copy(got_b[i][:], b_sb[i][:].indirect(n4_l[:]))
             else:
-                nc.vector.tensor_scalar(b_sb[i][:], acc["b", i][:], 0.0625, None, MULT)
+                nc.vector.tensor_tensor(got_b[i][:], b_sb[i][:].indirect(n4_l[:]), half_a[i][:], ADD)
 
         def finish(i):
-            got_b = ring.tile([P, W], F32, name="got_b")
-            if i in (0, C // P - 1):
-                nc.vector.tensor_copy(got_b[:], b_sb[i][:].indirect(n4_l[:]))
-                nc.vector.tensor_tensor(a_sb[i][:].indirect(n3_l[:]), got_b[:], half_a[i][:], ADD)
+            if i in on_vector:
+                nc.vector.tensor_tensor(a_sb[i][:].indirect(n3_l[:]), got_b[i][:], half_a[i][:], ADD)
             else:
-                nc.vector.tensor_tensor(got_b[:], b_sb[i][:].indirect(n4_l[:]), half_a[i][:], ADD)
-                nc.scalar.activation(a_sb[i][:].indirect(n3_l[:]), got_b[:], COPY)
-            nc.sync.dma_start(out[blocks[i], :], a_sb[i][:])
+                nc.scalar.activation(a_sb[i][:].indirect(n3_l[:]), got_b[i][:], COPY)
+            queue = nc.scalar if i == 2 else nc.sync
+            queue.dma_start(out[blocks[i], :], a_sb[i][:])
 
         copy_a(0)
         fetch_a(0)
         copy_b(0)
+        fetch_b(0)
+        copy_b(2)
         finish(0)
         copy_a(1)
-        copy_b(1)
         fetch_a(1)
+        copy_b(1)
         for i in (2, 3):
             copy_a(i)
         for i in (2, 3):
             fetch_a(i)
+        fetch_b(1)
+        copy_b(3)
         finish(1)
-        for i in (2, 3):
-            copy_b(i)
-        for i in (2, 3):
-            finish(i)
+        fetch_b(2)
+        fetch_b(3)
+        finish(2)
+        finish(3)

from contextlib import ExitStack

import concourse.mybir as mybir

K, T, S, H, W, C = 512, 2048, 512, 512, 256, 512
FLOPS = 3 * 2 * 512 * 512 * 512

F32 = mybir.dt.float32
BF16 = mybir.dt.bfloat16
I32 = mybir.dt.int32
U32 = mybir.dt.uint32
U16 = mybir.dt.uint16
U8 = mybir.dt.uint8
FP8X4 = mybir.dt.float8_e4m3fn_x4
COPY = mybir.ActivationFunctionType.Copy
ADD = mybir.AluOpType.add
MULT = mybir.AluOpType.mult

P = 128
PACK = 4
ROW_ORDER = (0, 2, 3, 1)
V_COLS = 344


def tile_picked_cdhputbhaar_none_p_kernel(
    tc, x_words, x_scales, w1, gs, offs, n1, n2, ca, hc, n3, n4, out
):
    nc = tc.nc
    with ExitStack() as ctx:
        keep = ctx.enter_context(tc.tile_pool(name="keep", bufs=1))
        ring = ctx.enter_context(tc.tile_pool(name="ring", bufs=4))
        psum = ctx.enter_context(tc.psum_pool(name="psum", bufs=1))

        def load_list(src, name):
            lst = keep.tile(list(src.shape), U16, name=name)
            nc.sync.dma_start(lst[:], src)
            return lst

        offs_l = load_list(offs, "offs_l")
        hc_l = load_list(hc, "hc_l")
        scale_table = keep.tile([P, T], U8, name="scale_table", align_bytes=64)
        table = scale_table[:].bitcast(I32)
        nc.vector.memset(table, 0)
        rows = x_scales[0].bitcast(I32)
        for s in range(2):
            nc.scalar.dma_start(table[s:P:16, :], rows[s:16:2, :])
        for s in range(2, 4):
            nc.sync.dma_start(table[s:P:32, :], rows[s:16:4, :])
        w_rows = w1.rearrange("(p j) c -> p j c", j=PACK)
        w_raw = []
        for h in range(2):
            part = keep.tile([P, PACK, H // 2], F32, name=f"w_raw{h}")
            nc.sync.dma_start(part[:], w_rows[:, :, h * (H // 2) : (h + 1) * (H // 2)])
            w_raw.append(part)
        ca_l = load_list(ca, "ca_l")
        word_table = keep.tile([P, T], U32, name="word_table", align_bytes=64)
        nc.sync.dma_start(
            word_table[:].bitcast(I32), x_words[0].rearrange("p n t -> p (n t)").bitcast(I32)
        )
        gain = keep.tile([P, PACK], F32, name="gain")
        nc.sync.dma_start(gain[:], gs.rearrange("(p t) o -> p (t o)", t=PACK))
        n1_l = load_list(n1, "n1_l")
        n2_l = load_list(n2, "n2_l")
        n3_l = load_list(n3, "n3_l")
        n4_l = load_list(n4, "n4_l")

        def pick(source, lst, dtype, name, pieces=1):
            got = keep.tile([P, S], dtype, name=name, align_bytes=64)
            return gather(got, source, lst, pieces)

        def gather(got, source, lst, pieces=1):
            n = S // pieces
            for i in range(pieces):
                nc.vector.tensor_copy(
                    got[:, i * n : (i + 1) * n],
                    source[:].indirect(lst[:, i * n // 16 : (i + 1) * n // 16]),
                )
            return got

        xq_scales = pick(scale_table, offs_l, U8, "xq_scales")
        hc_picked = pick(scale_table, hc_l, U8, "hc_picked")
        ca_scales = pick(scale_table, ca_l, U8, "ca_scales")

        hc_scales = keep.tile([P, C], U8, name="hc_scales", align_bytes=64)
        nc.vector.memset(hc_scales[:].bitcast(I32), 0)
        for r in range(4):
            first = r + 14 * (r // 2)
            nc.sync.dma_start(
                hc_scales[r:P:32, :].bitcast(I32), hc_picked[first:P:32, :].bitcast(I32)
            )

        w_bf = keep.tile([P, PACK, P, PACK], BF16, name="w_bf", tag="w_then_words", align_bytes=64)
        for h in range(2):
            nc.scalar.copy(
                w_bf[:, :, h * (P // 2) : (h + 1) * (P // 2), :].rearrange("p t m j -> p m j t"),
                w_raw[h][:].rearrange("p j (m t) -> p m j t", t=PACK),
            )
        w_words = keep.tile([P, H], U32, name="w_words", align_bytes=64)
        w_scales = keep.tile([P, H], U8, name="w_scales", align_bytes=64)
        w_flat = w_bf[:].rearrange("p t m j -> p (t m j)")
        for lo, hi in ((0, P), (P, H)):
            nc.vector.quantize_mx(
                out=w_words[:, lo:hi].bitcast(FP8X4),
                scales=w_scales[:, lo:hi],
                in_=w_flat[:, PACK * lo : PACK * hi],
            )
        xq_words = pick(word_table, offs_l, U32, "xq_words", pieces=2)
        cand_words = keep.tile([P, 2 * C], U32, name="cand_words", tag="w_then_words", align_bytes=64)
        ca_words = gather(cand_words[:, :C], word_table, ca_l)
        hc_words = gather(cand_words[:, C:], word_table, hc_l)

        halves = (slice(0, S // 2), slice(S // 2, S))
        whole = (slice(0, S),)

        def product(acc, words, scales, cols, mov_words, mov_scales, part):
            nc.tensor.matmul_mx(
                out=acc[:, part],
                lhsT=words[:, cols].bitcast(FP8X4),
                lhsT_scale=scales[:, cols],
                rhs=mov_words[:, part].bitcast(FP8X4),
                rhs_scale=mov_scales[:, part],
                start=True,
                stop=True,
            )

        def project(step):
            t = ROW_ORDER[step]
            cols = slice(t * P, (t + 1) * P)
            y = keep.tile([P, S], F32, name="y", tag=f"y{step}", align_bytes=64)
            for k, part in enumerate(halves if step == 0 else whole):
                y_ps = psum.tile([P, S], F32, name="y_ps", tag=f"y_ps{k}", bufs=1)
                product(y_ps, w_words, w_scales, cols, xq_words, xq_scales, part)
                nc.scalar.activation(y[:, part], y_ps[:, part], COPY, scale=gain[:, t : t + 1])
            pa = ring.tile([P, W], F32, name="pa")
            nc.scalar.activation(pa[:], y[:].indirect(n1_l[:]), COPY)
            neg_pb = ring.tile([P, W], F32, name="neg_pb")
            nc.scalar.activation(neg_pb[:], y[:].indirect(n2_l[:]), COPY, scale=-1.0)
            return pa, neg_pb

        def three_quarters(pair, tag):
            q = keep.tile([P, 2, W], F32, name="q", tag=tag, align_bytes=64)
            nc.scalar.activation(q[:, 0, :], pair[0][:], COPY, scale=0.75)
            nc.scalar.activation(q[:, 1, :], pair[1][:], COPY, scale=-0.75)
            return q

        pairs = [project(0)]
        sums = [three_quarters(pairs[0], "q0")]
        pairs.append(project(1))
        pairs.append(project(2))
        sums.append(three_quarters(pairs[1], "y2"))
        sums.append(three_quarters(pairs[2], "q2"))
        pairs.append(project(3))
        sums.append(three_quarters(pairs[3], "q3"))

        z_bf = keep.tile([P, S, PACK], BF16, name="z_bf", tag="y3", align_bytes=64)
        z_tiles = {}

        def put_differences(step):
            z = ring.tile([P, S], F32, name="z", bufs=3)
            nc.vector.tensor_tensor(z[:].indirect(n2_l[:]), pairs[step][0][:], pairs[step][1][:], ADD)
            z_tiles[step] = z

        def put_sums(step):
            z, t = z_tiles[step], ROW_ORDER[step]
            nc.vector.tensor_tensor(z[:].indirect(n1_l[:]), sums[step][:, 0, :], sums[step][:, 1, :], ADD)
            if step < 3:
                nc.scalar.copy(z_bf[:, :, t], z[:])
            else:
                nc.vector.tensor_copy(z_bf[:, : S // 2, t], z[:, : S // 2])
                nc.vector.tensor_copy(z_bf[:, S // 2 : V_COLS, t], z[:, S // 2 : V_COLS])
                nc.scalar.copy(z_bf[:, V_COLS:, t], z[:, V_COLS:])

        put_differences(0)
        put_sums(0)
        put_differences(1)
        put_differences(2)
        put_sums(1)
        put_sums(2)
        put_differences(3)
        put_sums(3)

        z_words = keep.tile([P, S], U32, name="z_words", align_bytes=64)
        z_scales = keep.tile([P, S], U8, name="z_scales", align_bytes=64)
        for part in halves:
            nc.vector.quantize_mx(
                out=z_words[:, part].bitcast(FP8X4),
                scales=z_scales[:, part],
                in_=z_bf[:, part, :].rearrange("p s t -> p (s t)"),
            )

        blocks = [slice(i * P, (i + 1) * P) for i in range(C // P)]
        sides = {"a": (ca_words, ca_scales), "b": (hc_words, hc_scales)}
        acc = {}
        jobs = [("a", 0, part) for part in halves] + [("b", 0, part) for part in halves]
        jobs.extend((side, i, whole[0]) for side, i in (("a", 1), ("b", 2), ("b", 1), ("a", 2), ("a", 3), ("b", 3)))
        for k, (side, i, part) in enumerate(jobs):
            bank = psum.tile([P, S], F32, name="acc", tag=f"y_ps{k % 8}", bufs=1)
            product(bank, sides[side][0], sides[side][1], blocks[i], z_words, z_scales, part)
            acc.setdefault((side, i), []).append((bank, part))

        a_sb, b_sb, half_a = {}, {}, {}

        def copy_a(i):
            a_sb[i] = ring.tile([P, S], F32, name="a")
            for bank, part in acc["a", i]:
                nc.scalar.activation(a_sb[i][:, part], bank[:, part], COPY, scale=0.0625)

        def fetch_a(i):
            half_a[i] = ring.tile([P, W], F32, name="half")
            nc.scalar.activation(half_a[i][:], a_sb[i][:].indirect(n3_l[:]), COPY, scale=-0.5)

        def copy_b(i):
            b_sb[i] = ring.tile([P, S], F32, name="b", tag=f"b{i % 2}", bufs=1)
            for bank, part in acc["b", i]:
                if i == 1:
                    nc.scalar.activation(b_sb[i][:, part], bank[:, part], COPY, scale=0.0625)
                else:
                    nc.vector.tensor_scalar(b_sb[i][:, part], bank[:, part], 0.0625, None, MULT)

        got_b = {}
        on_vector = (0, C // P - 1)

        def fetch_b(i):
            got_b[i] = ring.tile([P, W], F32, name="got_b")
            if i in on_vector:
                nc.vector.tensor_copy(got_b[i][:], b_sb[i][:].indirect(n4_l[:]))
            else:
                nc.vector.tensor_tensor(got_b[i][:], b_sb[i][:].indirect(n4_l[:]), half_a[i][:], ADD)

        def finish(i):
            if i in on_vector:
                nc.vector.tensor_tensor(a_sb[i][:].indirect(n3_l[:]), got_b[i][:], half_a[i][:], ADD)
            else:
                nc.scalar.activation(a_sb[i][:].indirect(n3_l[:]), got_b[i][:], COPY)
            queue = nc.scalar if i == 2 else nc.sync
            queue.dma_start(out[blocks[i], :], a_sb[i][:])

        copy_a(0)
        fetch_a(0)
        copy_b(0)
        fetch_b(0)
        copy_b(2)
        finish(0)
        copy_a(1)
        fetch_a(1)
        copy_b(1)
        for i in (2, 3):
            copy_a(i)
        for i in (2, 3):
            fetch_a(i)
        fetch_b(1)
        copy_b(3)
        finish(1)
        fetch_b(2)
        fetch_b(3)
        finish(2)
        finish(3)
